import numpy as np
import ml_dtypes


def mxq(x, axis, fmt="e4m3"):
    dtype, down = {"e4m3": (ml_dtypes.float8_e4m3fn, 7), "e5m2": (ml_dtypes.float8_e5m2, 14)}[fmt]
    v = np.moveaxis(np.asarray(x, np.float32).astype(ml_dtypes.bfloat16).astype(np.float64), axis, -1)
    blocks = v.reshape(v.shape[:-1] + (-1, 32))
    amax = np.abs(blocks).max(-1, keepdims=True)
    byte = np.maximum(np.where(amax > 0, np.frexp(amax)[1] - 1 + 127, 0) - down, 1)
    scale = np.exp2(byte - 127.0)
    codes = (blocks / scale).astype(np.float32).astype(dtype).astype(np.float64)
    return np.moveaxis((codes * scale).reshape(v.shape), -1, axis)


WIDE = False


def mx_kscale(k):
    if not WIDE:
        return np.ones(k)
    levels = np.array([10, -10, 5, -5, 0])
    if k % 512:
        return np.exp2(np.random.permutation(np.resize(levels, k // 32))).repeat(32)
    a = np.empty((k // 512, 16))
    for p in range(k // 512):
        a[p, :8] = np.random.permutation(np.resize(levels, 8))
        for g in range(8):
            far = levels[np.abs(levels - a[p, g]) >= 10]
            a[p, g + 8] = far[np.random.randint(len(far))]
    return np.exp2(a.ravel()).repeat(32)


def f64(x):
    return np.asarray(x).astype(np.float64)


def striped(idx):
    return np.tile(idx.reshape(-1, 16).T, (8, 1)).astype(np.uint16)


def unstriped(offs):
    return offs[:16].T.reshape(-1).astype(np.int64)


E2M1 = np.array([0.0, 0.5, 1.0, 1.5, 2.0, 3.0, 4.0, 6.0, -0.0, -0.5, -1.0, -1.5, -2.0, -3.0, -4.0, -6.0])


def pack_weight(w, fmt):
    k, n = w.shape
    w = f64(np.asarray(w, np.float32).astype(ml_dtypes.bfloat16)).reshape(k // 32, 32, n)
    amax = np.abs(w).max(1)
    if fmt == "e4m3":
        byte = np.frexp(amax)[1] - 1 + 127 - 7
    else:
        mant, ex = np.frexp(amax / 6.0)
        byte = np.where(mant > 0.5, ex, ex - 1) + 127
    byte = np.clip(np.where(amax > 0, byte, 1), 1, 254)
    scaled = (w * np.exp2(127.0 - byte)[:, None, :]).reshape(k, n).astype(np.float32)
    by_word = np.ascontiguousarray(scaled.reshape(k // 512, 128, 4, n).transpose(0, 1, 3, 2))
    if fmt == "e4m3":
        words = by_word.astype(ml_dtypes.float8_e4m3fn).view(np.uint8)
    else:
        c = by_word.astype(ml_dtypes.float4_e2m1fn).view(np.uint8) & 0xF
        words = (c[..., 0::2] | (c[..., 1::2] << 4)).reshape(k // 512, 128, 2 * n)
    return np.ascontiguousarray(words), np.ascontiguousarray(byte.astype(np.uint8).reshape(k // 512, 16, n))


def unpack_weight(words, scales, fmt):
    g, _, n = scales.shape
    words = np.ascontiguousarray(words).reshape(g, 128, n, -1)
    if fmt == "e4m3":
        vals = words.view(ml_dtypes.float8_e4m3fn).astype(np.float64)
    else:
        nib = np.empty((g, 128, n, 4), np.uint8)
        nib[..., 0::2] = words & 0xF
        nib[..., 1::2] = words >> 4
        vals = E2M1[nib]
    vals = vals * np.repeat(np.exp2(scales.astype(np.float64) - 127.0), 8, axis=1)[..., None]
    return vals.transpose(0, 1, 3, 2).reshape(g * 512, n)


def gelu(v):
    return 0.5 * v * (1.0 + np.tanh(np.sqrt(2.0 / np.pi) * (v + 0.044715 * v**3)))


K, T, S, T2, H, P, N = 1024, 2048, 512, 2048, 1024, 1024, 512


def setup_inputs():
    n = np.random.standard_normal
    s, u = mx_kscale(K)[:, None], mx_kscale(H)[:, None]
    d = {}
    d["tab_words"], d["tab_scales"] = pack_weight(n((K, T)) * s, "e4m3")
    d["tab2_words"], d["tab2_scales"] = pack_weight(n((K, T)) * s, "e4m3")
    d["offs"] = striped(np.random.permutation(T)[:S])
    d["offs2"] = striped(np.random.permutation(T)[:S])
    perm = np.random.permutation(T2)
    d["offs3"] = striped(perm[:S])
    d["offs4"] = striped(perm[S:2 * S])
    d["offs5"] = striped(np.random.permutation(T2)[:P])
    d["w1_words"], d["w1_scales"] = pack_weight(2.2 * n((K, H)) / K**0.5 / s, "e2m1")
    d["b1"] = n(H).astype(np.float32)
    d["w2"] = (0.56 * n((K, H)) / K**0.5 / s).astype(np.float32)
    d["w3"] = (2.2 * n((K, H)) / K**0.5 / s).astype(np.float32)
    d["wg1"] = np.exp(0.3 * n((128, S))).astype(np.float32)
    d["wg2"] = np.exp(0.3 * n((128, S))).astype(np.float32)
    d["page0"] = (0.8 * n((H, T2))).astype(np.float32)
    d["gain"] = (np.exp(0.3 * n(H)) * u[:, 0]).astype(np.float32)
    d["w4_words"], d["w4_scales"] = pack_weight(1.8 * n((H, N)) / H**0.5 / u, "e4m3")
    d["cap"] = (0.8 * n((N, P)) + 0.5).astype(np.float32)
    return d


def reference(tab_words, tab_scales, tab2_words, tab2_scales, offs, offs2, offs3, offs4, offs5,
              w1_words, w1_scales, b1, w2, w3, wg1, wg2, page0, gain, w4_words, w4_scales, cap):
    v = unpack_weight(tab_words, tab_scales, "e4m3")[:, unstriped(offs)]
    v2 = unpack_weight(tab2_words, tab2_scales, "e4m3")[:, unstriped(offs2)]
    f1 = unpack_weight(w1_words, w1_scales, "e2m1").T @ v
    h1 = 1.0 / (1.0 + np.exp(-(f1 + f64(b1)[:, None])))
    ang = mxq(f64(w2), 0, "e4m3").T @ v2
    ext = mxq(f64(w3), 0, "e4m3").T @ v2
    h2 = np.sin(ang) * ext
    page = f64(page0).copy()
    page[:, unstriped(offs3)] = np.tile(f64(wg1), (H // 128, 1)) * h1
    page[:, unstriped(offs4)] = np.tile(f64(wg2), (H // 128, 1)) * h2
    x = page[:, unstriped(offs5)]
    x = 0.5 * x * (1.0 + np.tanh((2.0 / np.pi)**0.5 * (x + 0.044715 * x**3)))
    xq = mxq(x * f64(gain)[:, None], 0, "e4m3")
    y = unpack_weight(w4_words, w4_scales, "e4m3").T @ xq
    return np.minimum(y, f64(cap))

@@ -1,0 +1,331 @@
+import math
+from contextlib import ExitStack
+
+import concourse.mybir as mybir
+
+K, T, S, T2, H, M, N = 1024, 2048, 512, 2048, 1024, 1024, 512
+FLOPS = 2 * K * H * S * 3 + 2 * H * N * M
+
+F32 = mybir.dt.float32
+BF16 = mybir.dt.bfloat16
+I32 = mybir.dt.int32
+U32 = mybir.dt.uint32
+U16 = mybir.dt.uint16
+U8 = mybir.dt.uint8
+FP8X4 = mybir.dt.float8_e4m3fn_x4
+FP4X4 = mybir.dt.float4_e2m1fn_x4
+ACT = mybir.ActivationFunctionType
+ALU = mybir.AluOpType
+
+P = 128
+PACK = 4
+PASS = P * PACK
+PASSES = K // PASS
+HALVES = H // PASS
+TILES = H // P
+COLS = 512
+CHUNKS = M // COLS
+ROUNDER = 1.5 * 2.0**23
+TWO_PI = 2.0 * math.pi
+
+
+def tile_list_sawmill_slot_scores_kernel(
+    tc, tab_words, tab_scales, tab2_words, tab2_scales, offs, offs2, offs3, offs4, offs5,
+    w1_words, w1_scales, b1, w2, w3, wg1, wg2, page0, gain, w4_words, w4_scales, cap, out,
+):
+    nc = tc.nc
+    with ExitStack() as ctx:
+        lists = ctx.enter_context(tc.tile_pool(name="lists", bufs=1))
+        sb = ctx.enter_context(tc.tile_pool(name="sb", bufs=1))
+        ps = ctx.enter_context(tc.psum_pool(name="ps", bufs=1))
+
+        def tile(shape, dtype, tag):
+            return sb.tile(shape, dtype, tag=tag, name=tag, align_bytes=64)
+
+        def bank(i):
+            return ps.tile([P, COLS], F32, tag="bank%d" % i, name="bank%d" % i)
+
+        def load_list(src, name):
+            t = lists.tile(list(src.shape), U16, name=name)
+            nc.sync.dma_start(t[:], src)
+            return t
+
+        def load_words(words, a, tag):
+            t = tile([P, words.shape[2]], I32, tag)
+            nc.sync.dma_start(t[:], words[a].rearrange("p c i -> p (c i)").bitcast(I32))
+            return t
+
+        def load_planes_side_by_side(queue, planes, scales):
+            for q in range(4):
+                queue.dma_start(
+                    planes[32 * q : 32 * q + 4, :].bitcast(I32).rearrange("r (a c) -> r a c", a=PASSES),
+                    scales[:, 4 * q : 4 * q + 4, :].bitcast(I32).rearrange("a r c -> r a c"),
+                )
+
+        def load_planes_packed(queue, planes, scales):
+            for q in range(4):
+                queue.dma_start(
+                    planes[32 * q : 32 * q + 4 * PASSES, :].bitcast(I32),
+                    scales[:, 4 * q : 4 * q + 4, :].bitcast(I32),
+                )
+
+        def load_wg(wg, tag):
+            t = tile([P, PACK, S], F32, tag)
+            for q in (0, 2, 1, 3):
+                nc.sync.dma_start(t[32 * q : 32 * q + 32, :, :], wg.rearrange("(q t) j -> q t j", t=PACK))
+            return t
+
+        def load_per_row(vec, tag):
+            t = tile([P, HALVES, PACK], F32, tag)
+            nc.sync.dma_start(t[:], vec.rearrange("(b p t) -> p b t", b=HALVES, t=PACK))
+            return t
+
+        def load_page(s, tag):
+            b, t = divmod(s, PACK)
+            pg = tile([P, T2], F32, tag)
+            nc.sync.dma_start(pg[:], page0[PASS * b : PASS * (b + 1), :].rearrange("(p t) c -> p t c", t=PACK)[:, t, :])
+            return pg
+
+        tab_planes = tile([P, PASSES * T], U8, "x4a")
+        nc.vector.memset(tab_planes[:].bitcast(I32), 0)
+        w1_planes = tile([P, PASSES * H], U8, "w1s")
+        nc.vector.memset(w1_planes[:].bitcast(I32), 0)
+        tab2_planes = tile([P, T], U8, "tab2s")
+        nc.vector.memset(tab2_planes[:].bitcast(I32), 0)
+        w4_planes = tile([P, N], U8, "w4s")
+        nc.vector.memset(w4_planes[:].bitcast(I32), 0)
+
+        idx = load_list(offs, "idx")
+        tab = [load_words(tab_words, 0, "big0")]
+        load_planes_side_by_side(nc.sync, tab_planes, tab_scales)
+        w1_raw = tile([P, PASSES * 2 * H], U8, "x4b")
+        nc.sync.dma_start(
+            w1_raw[:].bitcast(I32).rearrange("p (a c) -> p a c", a=PASSES),
+            w1_words.bitcast(I32).rearrange("a p c -> p a c"),
+        )
+        tab.append(load_words(tab_words, 1, "big1"))
+        load_planes_side_by_side(nc.sync, w1_planes, w1_scales)
+        b1_sb = load_per_row(b1, "b1")
+        idx3 = load_list(offs3, "idx3")
+        pages = [load_page(0, "page0")]
+        wg1_sb = load_wg(wg1, "wg1")
+
+        def gather_words(windows, offsets, name):
+            g = tile([P, PASSES * S], U32, name)
+            for a in range(PASSES):
+                nc.vector.tensor_copy(g[:, S * a : S * (a + 1)], windows[a][:].bitcast(U32).indirect(offsets[:]))
+            return g
+
+        w1_codes = tile([P, HALVES, PASSES, 2 * PASS], U8, "wbf0")
+        w1_bytes = tile([P, HALVES, PASSES, PASS], U8, "wbf2")
+
+        def deal_w1(b):
+            nc.vector.tensor_copy(
+                w1_codes[:, b].bitcast(U16).rearrange("p a (t m) -> p a t m", t=PACK),
+                w1_raw[:].bitcast(U16).rearrange("p (a b m t) -> p b a t m", a=PASSES, b=HALVES, t=PACK)[:, b],
+            )
+            nc.vector.tensor_copy(
+                w1_bytes[:, b].rearrange("p a (t m) -> p a t m", t=PACK),
+                w1_planes[:].rearrange("p (a b m t) -> p b a t m", a=PASSES, b=HALVES, t=PACK)[:, b],
+            )
+
+        deal_w1(0)
+        v_words = gather_words(tab, idx, "wbf1")
+        v_planes = []
+        for a in range(PASSES):
+            g = tile([P, S], U8, "vs%d" % a)
+            nc.vector.tensor_copy(g[:], tab_planes[:, a * T : (a + 1) * T].indirect(idx[:]))
+            v_planes.append(g)
+        deal_w1(1)
+
+        h1, f1s = [], []
+        for s in range(TILES):
+            b, t = divmod(s, PACK)
+            f1 = bank(s)
+            for a in range(PASSES):
+                nc.tensor.matmul_mx(
+                    f1[:],
+                    lhsT=w1_codes[:, b, a, 2 * P * t : 2 * P * (t + 1)].bitcast(FP4X4),
+                    lhsT_scale=w1_bytes[:, b, a, P * t : P * (t + 1)],
+                    rhs=v_words[:, S * a : S * (a + 1)].bitcast(FP8X4),
+                    rhs_scale=v_planes[a][:],
+                    start=(a == 0),
+                    stop=(a == PASSES - 1),
+                )
+            f1s.append(f1)
+
+        def profile_features(s, tag):
+            b, t = divmod(s, PACK)
+            h = tile([P, S], F32, tag)
+            nc.scalar.activation(h[:], f1s[s][:], ACT.Sigmoid, bias=b1_sb[:, b, t : t + 1])
+            h1.append(h)
+
+        for s in range(TILES):
+            profile_features(s, "h%d" % s)
+
+        def put_h1(s):
+            nc.vector.tensor_tensor(pages[s][:].indirect(idx3[:]), h1[s][:], wg1_sb[:, s % PACK, :], ALU.mult)
+
+        def load_raw(w, a, b, tag):
+            raw = tile([P, PACK, PASS], F32, tag)
+            nc.sync.dma_start(
+                raw[:], w[PASS * a : PASS * (a + 1), PASS * b : PASS * (b + 1)].rearrange("(p j) c -> p j c", j=PACK)
+            )
+            return raw
+
+        def quantise_weight(raw, slot, name):
+            rounded = tile([P, PASS * PACK], BF16, "wbf%d" % slot)
+            nc.scalar.copy(
+                rounded[:].rearrange("p (t m j) -> p m t j", t=PACK, j=PACK),
+                raw[:].rearrange("p j (m t) -> p m t j", t=PACK),
+            )
+            codes = tile([P, PASS], U32, name + "c")
+            plane = tile([P, PASS], U8, name + "s")
+            nc.vector.quantize_mx(codes[:].bitcast(FP8X4), plane[:], rounded[:])
+            return codes, plane
+
+        def product(acc, weight, t):
+            for a in range(PASSES):
+                codes, plane = weight[a]
+                nc.tensor.matmul_mx(
+                    acc[:],
+                    lhsT=codes[:, P * t : P * (t + 1)].bitcast(FP8X4),
+                    lhsT_scale=plane[:, P * t : P * (t + 1)],
+                    rhs=v2_words[:, S * a : S * (a + 1)].bitcast(FP8X4),
+                    rhs_scale=v2_planes[4 * a : P, :],
+                    start=(a == 0),
+                    stop=(a == PASSES - 1),
+                )
+
+        sine_tags = ["h0", "g1", "g2", "h3", "h4", "h5", "h6", "h7"]
+
+        def sines(b, w2q):
+            got = []
+            for t in range(PACK):
+                ang = bank(t)
+                product(ang, w2q, t)
+                shifted = tile([P, S], U32, "u%d" % (t % 2))
+                nc.scalar.activation(shifted[:], ang[:], ACT.Copy, bias=ROUNDER, scale=1.0 / TWO_PI)
+                turns = tile([P, S], F32, "k%d" % (t % 2))
+                nc.scalar.activation(turns[:], shifted[:], ACT.Copy, bias=-ROUNDER)
+                reduced = tile([P, S], F32, "r%d" % (t % 2))
+                nc.vector.scalar_tensor_tensor(reduced[:], turns[:], -TWO_PI, ang[:], ALU.mult, ALU.add)
+                sine = tile([P, S], F32, sine_tags[PACK * b + t])
+                nc.scalar.activation(sine[:], reduced[:], ACT.Sin)
+                got.append(sine)
+            return got
+
+        h2 = {}
+
+        def extents(w3q):
+            got = []
+            for t in range(PACK):
+                ext = bank(PACK + t)
+                product(ext, w3q, t)
+                got.append(ext)
+            return got
+
+        def knot_features(s, ext, sine, tag=None):
+            h2[s] = sine if tag is None else tile([P, S], F32, tag)
+            nc.vector.tensor_tensor(h2[s][:], ext[:], sine[:], ALU.mult)
+
+        put_h1(0)
+        pages.append(load_page(1, "page1"))
+        put_h1(1)
+        pages.append(load_page(2, "page2"))
+        put_h1(2)
+        idx2 = load_list(offs2, "idx2")
+        tab2 = [load_words(tab2_words, 0, "big2")]
+        load_planes_packed(nc.sync, tab2_planes, tab2_scales)
+        tab2.append(load_words(tab2_words, 1, "big3"))
+        v2_words = gather_words(tab2, idx2, "h1")
+        v2_planes = tile([P, S], U8, "h2")
+        nc.vector.tensor_copy(v2_planes[:], tab2_planes[:].indirect(idx2[:]))
+        pages.append(load_page(3, "page3"))
+        put_h1(3)
+
+        raw2 = [load_raw(w2, a, 0, "raw%d" % a) for a in range(PASSES)]
+        pages.append(load_page(4, "page4"))
+        raw3 = [load_raw(w3, 0, 0, "raw2")]
+        pages.append(load_page(5, "page5"))
+        raw3.append(load_raw(w3, 1, 0, "raw3"))
+        idx4 = load_list(offs4, "idx4")
+        idx5 = load_list(offs5, "idx5")
+        gain_sb = load_per_row(gain, "gain")
+        load_planes_packed(nc.sync, w4_planes, w4_scales)
+        put_h1(4)
+        put_h1(5)
+        w2q = [quantise_weight(raw2[a], a, "w2q0%d" % a) for a in range(PASSES)]
+        pages.append(load_page(6, "raw0"))
+        pages.append(load_page(7, "raw1"))
+        sine = sines(0, w2q)
+        w3q = [quantise_weight(raw3[a], (2, 0)[a], "w3q0%d" % a) for a in range(PASSES)]
+        wg2_sb = load_wg(wg2, "raw2")
+        put_h1(6)
+        put_h1(7)
+        ext = extents(w3q)
+        knot_features(0, ext[0], sine[0])
+        knot_features(3, ext[3], sine[3])
+        raw2 = [load_raw(w2, a, 1, ("raw3", "wg1")[a]) for a in range(PASSES)]
+        w2q = [quantise_weight(raw2[a], (1, 2)[a], "w2q1%d" % a) for a in range(PASSES)]
+        knot_features(1, ext[1], sine[1], "wbf2")
+        raw3 = [load_raw(w3, a, 1, ("raw3", "wg1")[a]) for a in range(PASSES)]
+        w3q = [quantise_weight(raw3[a], a, "w3q1%d" % a) for a in range(PASSES)]
+        knot_features(2, ext[2], sine[2], "wbf1")
+        sine = sines(1, w2q)
+        ext = extents(w3q)
+        for t in range(PACK):
+            knot_features(PACK + t, ext[t], sine[t])
+        caps = []
+        for c in range(CHUNKS):
+            t = tile([P, N // P, COLS], F32, ("raw3", "wg1")[c])
+            nc.sync.dma_start(t[:], cap[:, COLS * c : COLS * (c + 1)].rearrange("(n p) m -> p n m", p=P))
+            caps.append(t)
+        w4_codes = tile([P, HALVES, N], U32, "h1")
+        nc.sync.dma_start(w4_codes[:].bitcast(I32), w4_words.rearrange("a p c i -> p a (c i)").bitcast(I32))
+
+        picked_tags = ["big2", "pk0", "pk1", "big3", "wbf0", "wbf2", "wbf1", "big3"]
+        scores = {}
+        count = 0
+        for b in range(HALVES):
+            planes = tile([P, PACK, M], BF16, "big%d" % b)
+            for t in range(PACK):
+                s = PACK * b + t
+                nc.vector.tensor_tensor(pages[s][:].indirect(idx4[:]), h2[s][:], wg2_sb[:, t, :], ALU.mult)
+                picked = tile([P, M], F32, picked_tags[s])
+                parts = [slice(0, M)] if s < TILES - 1 else [slice(COLS * c, COLS * (c + 1)) for c in range(CHUNKS)]
+                for part in parts:
+                    nc.vector.tensor_copy(
+                        picked[:, part], pages[s][:].indirect(idx5[:, part.start // 16 : part.stop // 16])
+                    )
+                    act = tile([P, part.stop - part.start], F32, ("r1", "big2")[count % 2])
+                    count = count + 1
+                    nc.scalar.activation(act[:], picked[:, part], ACT.Gelu_apprx_tanh)
+                    nc.scalar.activation(planes[:, t, part], act[:], ACT.Copy, scale=gain_sb[:, b, t : t + 1])
+            for c in range(CHUNKS):
+                woven = tile([P, COLS * PACK], BF16, ("x4a", "x4b")[c])
+                dst = woven[:].rearrange("p (c i t) -> p c t i", i=4, t=PACK)
+                src = planes[:, :, COLS * c : COLS * (c + 1)].rearrange("p t (c i) -> p c t i", i=4)
+                if b == HALVES - 1 and c == 0:
+                    nc.vector.tensor_copy(dst, src)
+                else:
+                    nc.scalar.copy(dst, src)
+                name = "w%dq0%d" % (2 + b, c)
+                codes = tile([P, COLS], U32, name + "c")
+                plane = tile([P, COLS], U8, name + "s")
+                nc.vector.quantize_mx(codes[:].bitcast(FP8X4), plane[:], woven[:])
+                for n in range(N // P):
+                    if b == 0:
+                        scores[c, n] = bank(PACK * c + n)
+                    nc.tensor.matmul_mx(
+                        scores[c, n][:],
+                        lhsT=w4_codes[:, b, P * n : P * (n + 1)].bitcast(FP8X4),
+                        lhsT_scale=w4_planes[4 * b : P, P * n : P * (n + 1)],
+                        rhs=codes[:].bitcast(FP8X4),
+                        rhs_scale=plane[:],
+                        start=(b == 0),
+                        stop=(b == HALVES - 1),
+                    )
+                    if b == HALVES - 1:
+                        nc.vector.tensor_tensor(caps[c][:, n, :], scores[c, n][:], caps[c][:, n, :], ALU.min)
+                        nc.sync.dma_start(out[P * n : P * (n + 1), COLS * c : COLS * (c + 1)], caps[c][:, n, :])

@@ -2,6 +2,7 @@ import math
 from contextlib import ExitStack
 
 import concourse.mybir as mybir
+from concourse.masks import make_identity
 
 K, T, S, T2, H, M, N = 1024, 2048, 512, 2048, 1024, 1024, 512
 FLOPS = 2 * K * H * S * 3 + 2 * H * N * M
@@ -62,18 +63,34 @@ def tile_list_sawmill_slot_scores_kernel(
                     scales[:, 4 * q : 4 * q + 4, :].bitcast(I32).rearrange("a r c -> r a c"),
                 )
 
-        def load_planes_packed(queue, planes, scales):
-            for q in range(4):
-                queue.dma_start(
-                    planes[32 * q : 32 * q + 4 * PASSES, :].bitcast(I32),
-                    scales[:, 4 * q : 4 * q + 4, :].bitcast(I32),
-                )
+        def load_planes_packed(planes, scales, q):
+            nc.sync.dma_start(
+                planes[32 * q : 32 * q + 4 * PASSES, :].bitcast(I32),
+                scales[:, 4 * q : 4 * q + 4, :].bitcast(I32),
+            )
 
         def load_wg(wg, tag):
-            t = tile([P, PACK, S], F32, tag)
-            for q in (0, 2, 1, 3):
-                nc.sync.dma_start(t[32 * q : 32 * q + 32, :, :], wg.rearrange("(q t) j -> q t j", t=PACK))
+            t = tile([P, S], F32, tag)
+            nc.sync.dma_start(t[:], wg)
             return t
+
+        def deal_wg(rows, tag, first_bank):
+            turned = bank(first_bank)
+            for jb in range(PACK):
+                nc.tensor.transpose(turned[:, P * jb : P * (jb + 1)], rows[:, P * jb : P * (jb + 1)], ident[:])
+            spread = tile([P, PACK, PACK, P], F32, "turns")
+            for t in range(PACK):
+                nc.scalar.copy(
+                    spread[:, t].rearrange("p jb (a q) -> p jb a q", a=4),
+                    turned[:].rearrange("p (jb q t) -> p t jb q", jb=PACK, t=PACK)[:, t].unsqueeze(2).to_broadcast([P, PACK, 4, 32]),
+                )
+            dealt = tile([P, PACK, S], F32, tag)
+            for t in range(PACK):
+                back = bank((first_bank + 1 + t) % 8)
+                for jb in range(PACK):
+                    nc.tensor.transpose(back[:, P * jb : P * (jb + 1)], spread[:, t, jb, :], ident[:])
+                nc.scalar.copy(dealt[:, t, :], back[:])
+            return dealt
 
         def load_per_row(vec, tag):
             t = tile([P, HALVES, PACK], F32, tag)
@@ -86,6 +103,10 @@ def tile_list_sawmill_slot_scores_kernel(
             nc.sync.dma_start(pg[:], page0[PASS * b : PASS * (b + 1), :].rearrange("(p t) c -> p t c", t=PACK)[:, t, :])
             return pg
 
+        ident = tile([P, P], F32, "ident")
+        make_identity(nc, ident[:])
+        warm = tile([P, 1], F32, "warm")
+        nc.scalar.activation(warm[:], ident[:, 0:1], ACT.Sigmoid)
         tab_planes = tile([P, PASSES * T], U8, "x4a")
         nc.vector.memset(tab_planes[:].bitcast(I32), 0)
         w1_planes = tile([P, PASSES * H], U8, "w1s")
@@ -96,19 +117,26 @@ def tile_list_sawmill_slot_scores_kernel(
         nc.vector.memset(w4_planes[:].bitcast(I32), 0)
 
         idx = load_list(offs, "idx")
+        wg1_rows = load_wg(wg1, "wg1n")
         tab = [load_words(tab_words, 0, "big0")]
         load_planes_side_by_side(nc.sync, tab_planes, tab_scales)
-        w1_raw = tile([P, PASSES * 2 * H], U8, "x4b")
-        nc.sync.dma_start(
-            w1_raw[:].bitcast(I32).rearrange("p (a c) -> p a c", a=PASSES),
-            w1_words.bitcast(I32).rearrange("a p c -> p a c"),
-        )
+
+        def load_w1(b, tag):
+            t = tile([P, PASSES * 2 * PASS], U8, tag)
+            nc.sync.dma_start(
+                t[:].bitcast(I32).rearrange("p (a c) -> p a c", a=PASSES),
+                w1_words[:, :, 2 * PASS * b : 2 * PASS * (b + 1)].bitcast(I32).rearrange("a p c -> p a c"),
+            )
+            return t
+
+        w1_raw = [load_w1(0, "x4b")]
         tab.append(load_words(tab_words, 1, "big1"))
         load_planes_side_by_side(nc.sync, w1_planes, w1_scales)
         b1_sb = load_per_row(b1, "b1")
         idx3 = load_list(offs3, "idx3")
         pages = [load_page(0, "page0")]
-        wg1_sb = load_wg(wg1, "wg1")
+        w1_raw.append(load_w1(1, "pk0"))
+        wg1_sb = deal_wg(wg1_rows, "wg1", 0)
 
         def gather_words(windows, offsets, name):
             g = tile([P, PASSES * S], U32, name)
@@ -122,7 +150,7 @@ def tile_list_sawmill_slot_scores_kernel(
         def deal_w1(b):
             nc.vector.tensor_copy(
                 w1_codes[:, b].bitcast(U16).rearrange("p a (t m) -> p a t m", t=PACK),
-                w1_raw[:].bitcast(U16).rearrange("p (a b m t) -> p b a t m", a=PASSES, b=HALVES, t=PACK)[:, b],
+                w1_raw[b][:].bitcast(U16).rearrange("p (a m t) -> p a t m", a=PASSES, t=PACK),
             )
             nc.vector.tensor_copy(
                 w1_bytes[:, b].rearrange("p a (t m) -> p a t m", t=PACK),
@@ -138,10 +166,10 @@ def tile_list_sawmill_slot_scores_kernel(
             v_planes.append(g)
         deal_w1(1)
 
-        h1, f1s = [], []
+        h1, f1s = {}, []
         for s in range(TILES):
             b, t = divmod(s, PACK)
-            f1 = bank(s)
+            f1 = bank((s + 5) % 8)
             for a in range(PASSES):
                 nc.tensor.matmul_mx(
                     f1[:],
@@ -158,9 +186,9 @@ def tile_list_sawmill_slot_scores_kernel(
             b, t = divmod(s, PACK)
             h = tile([P, S], F32, tag)
             nc.scalar.activation(h[:], f1s[s][:], ACT.Sigmoid, bias=b1_sb[:, b, t : t + 1])
-            h1.append(h)
+            h1[s] = h
 
-        for s in range(TILES):
+        for s in (0, 1, 2, 4, 5, 6, 7):
             profile_features(s, "h%d" % s)
 
         def put_h1(s):
@@ -173,12 +201,18 @@ def tile_list_sawmill_slot_scores_kernel(
             )
             return raw
 
-        def quantise_weight(raw, slot, name):
+        def quantise_weight(raw, slot, name, dealt):
             rounded = tile([P, PASS * PACK], BF16, "wbf%d" % slot)
-            nc.scalar.copy(
-                rounded[:].rearrange("p (t m j) -> p m t j", t=PACK, j=PACK),
-                raw[:].rearrange("p j (m t) -> p m t j", t=PACK),
-            )
+            if dealt:
+                nc.scalar.copy(
+                    rounded[:].rearrange("p (t m j) -> p m t j", t=PACK, j=PACK),
+                    raw[:].rearrange("p j (m t) -> p m t j", t=PACK),
+                )
+            else:
+                nc.scalar.copy(
+                    rounded[:].rearrange("p (c i j) -> p c j i", i=4, j=PACK),
+                    raw[:].rearrange("p j (c i) -> p c j i", i=4),
+                )
             codes = tile([P, PASS], U32, name + "c")
             plane = tile([P, PASS], U8, name + "s")
             nc.vector.quantize_mx(codes[:].bitcast(FP8X4), plane[:], rounded[:])
@@ -200,27 +234,47 @@ def tile_list_sawmill_slot_scores_kernel(
         sine_tags = ["h0", "g1", "g2", "h3", "h4", "h5", "h6", "h7"]
 
         def sines(b, w2q):
+            turns = tile([P, PACK, PACK, P], F32, "turns")
+            whole = tile([P, PACK, PACK, P], F32, "whole")
+            for jb in range(PACK):
+                ang = bank(jb)
+                for a in range(PASSES):
+                    codes, plane = w2q[a]
+                    nc.tensor.matmul_mx(
+                        ang[:],
+                        lhsT=v2_words[:, S * a + P * jb : S * a + P * (jb + 1)].bitcast(FP8X4),
+                        lhsT_scale=v2_planes[4 * a : P, P * jb : P * (jb + 1)],
+                        rhs=codes[:].bitcast(FP8X4),
+                        rhs_scale=plane[:],
+                        start=(a == 0),
+                        stop=(a == PASSES - 1),
+                    )
+                nc.scalar.activation(
+                    turns[:, jb], ang[:].rearrange("p (m t) -> p t m", t=PACK), ACT.Copy, scale=1.0 / TWO_PI
+                )
+                shifted = tile([P, PACK, P], U32, "u%d" % (jb % 2))
+                nc.scalar.activation(shifted[:], turns[:, jb], ACT.Copy, bias=ROUNDER)
+                nc.scalar.activation(whole[:, jb], shifted[:], ACT.Copy, bias=ROUNDER, scale=-1.0)
             got = []
             for t in range(PACK):
-                ang = bank(t)
-                product(ang, w2q, t)
-                shifted = tile([P, S], U32, "u%d" % (t % 2))
-                nc.scalar.activation(shifted[:], ang[:], ACT.Copy, bias=ROUNDER, scale=1.0 / TWO_PI)
-                turns = tile([P, S], F32, "k%d" % (t % 2))
-                nc.scalar.activation(turns[:], shifted[:], ACT.Copy, bias=-ROUNDER)
-                reduced = tile([P, S], F32, "r%d" % (t % 2))
-                nc.vector.scalar_tensor_tensor(reduced[:], turns[:], -TWO_PI, ang[:], ALU.mult, ALU.add)
+                rest = bank(t)
+                for jb in range(PACK):
+                    for k, term in enumerate((turns, whole)):
+                        nc.tensor.matmul(
+                            rest[:, P * jb : P * (jb + 1)], lhsT=term[:, jb, t, :], rhs=ident[:],
+                            start=(k == 0), stop=(k == 1), is_transpose=True,
+                        )
                 sine = tile([P, S], F32, sine_tags[PACK * b + t])
-                nc.scalar.activation(sine[:], reduced[:], ACT.Sin)
+                nc.scalar.activation(sine[:], rest[:], ACT.Sin, scale=TWO_PI)
                 got.append(sine)
             return got
 
         h2 = {}
 
-        def extents(w3q):
+        def extents(w3q, first_bank):
             got = []
             for t in range(PACK):
-                ext = bank(PACK + t)
+                ext = bank(first_bank + t)
                 product(ext, w3q, t)
                 got.append(ext)
             return got
@@ -230,65 +284,70 @@ def tile_list_sawmill_slot_scores_kernel(
             nc.vector.tensor_tensor(h2[s][:], ext[:], sine[:], ALU.mult)
 
         put_h1(0)
+        load_planes_packed(tab2_planes, tab2_scales, 0)
         pages.append(load_page(1, "page1"))
         put_h1(1)
+        wg2_rows = load_wg(wg2, "wg2n")
+        wg2_sb = deal_wg(wg2_rows, "wg2", 4)
+        load_planes_packed(tab2_planes, tab2_scales, 1)
         pages.append(load_page(2, "page2"))
         put_h1(2)
         idx2 = load_list(offs2, "idx2")
+        load_planes_packed(tab2_planes, tab2_scales, 2)
         tab2 = [load_words(tab2_words, 0, "big2")]
-        load_planes_packed(nc.sync, tab2_planes, tab2_scales)
+        load_planes_packed(tab2_planes, tab2_scales, 3)
         tab2.append(load_words(tab2_words, 1, "big3"))
         v2_words = gather_words(tab2, idx2, "h1")
         v2_planes = tile([P, S], U8, "h2")
         nc.vector.tensor_copy(v2_planes[:], tab2_planes[:].indirect(idx2[:]))
-        pages.append(load_page(3, "page3"))
-        put_h1(3)
 
         raw2 = [load_raw(w2, a, 0, "raw%d" % a) for a in range(PASSES)]
+        pages.append(load_page(3, "page3"))
         pages.append(load_page(4, "page4"))
         raw3 = [load_raw(w3, 0, 0, "raw2")]
         pages.append(load_page(5, "page5"))
         raw3.append(load_raw(w3, 1, 0, "raw3"))
+        pages.append(load_page(6, "big0"))
         idx4 = load_list(offs4, "idx4")
+        pages.append(load_page(7, "big1"))
         idx5 = load_list(offs5, "idx5")
-        gain_sb = load_per_row(gain, "gain")
-        load_planes_packed(nc.sync, w4_planes, w4_scales)
-        put_h1(4)
-        put_h1(5)
-        w2q = [quantise_weight(raw2[a], a, "w2q0%d" % a) for a in range(PASSES)]
-        pages.append(load_page(6, "raw0"))
-        pages.append(load_page(7, "raw1"))
+        w2q = [quantise_weight(raw2[a], a, "w2q0%d" % a, False) for a in range(PASSES)]
+        profile_features(3, "wbf0")
         sine = sines(0, w2q)
-        w3q = [quantise_weight(raw3[a], (2, 0)[a], "w3q0%d" % a) for a in range(PASSES)]
-        wg2_sb = load_wg(wg2, "raw2")
-        put_h1(6)
-        put_h1(7)
-        ext = extents(w3q)
+        put_h1(3)
+        put_h1(4)
+        w3q = [quantise_weight(raw3[a], (2, 1)[a], "w3q0%d" % a, True) for a in range(PASSES)]
+        for s in range(5, TILES):
+            put_h1(s)
+        ext = extents(w3q, PACK)
         knot_features(0, ext[0], sine[0])
-        knot_features(3, ext[3], sine[3])
-        raw2 = [load_raw(w2, a, 1, ("raw3", "wg1")[a]) for a in range(PASSES)]
-        w2q = [quantise_weight(raw2[a], (1, 2)[a], "w2q1%d" % a) for a in range(PASSES)]
-        knot_features(1, ext[1], sine[1], "wbf2")
-        raw3 = [load_raw(w3, a, 1, ("raw3", "wg1")[a]) for a in range(PASSES)]
-        w3q = [quantise_weight(raw3[a], a, "w3q1%d" % a) for a in range(PASSES)]
-        knot_features(2, ext[2], sine[2], "wbf1")
+        knot_features(1, ext[1], sine[1])
+        raw2 = [load_raw(w2, a, 1, "raw%d" % a) for a in range(PASSES)]
+        gain_sb = load_per_row(gain, "gain")
+        raw3 = [load_raw(w3, a, 1, "raw%d" % (2 + a)) for a in range(PASSES)]
+        w2q = [quantise_weight(raw2[a], (0, 2)[a], "w2q1%d" % a, False) for a in range(PASSES)]
+        knot_features(2, ext[2], sine[2], "wbf2")
+        w3q = [quantise_weight(raw3[a], (1, 3)[a], "w3q1%d" % a, True) for a in range(PASSES)]
+        knot_features(3, ext[3], sine[3], "wbf3")
         sine = sines(1, w2q)
-        ext = extents(w3q)
+        ext = extents(w3q, 0)
         for t in range(PACK):
             knot_features(PACK + t, ext[t], sine[t])
+        for q in range(4):
+            load_planes_packed(w4_planes, w4_scales, q)
         caps = []
         for c in range(CHUNKS):
-            t = tile([P, N // P, COLS], F32, ("raw3", "wg1")[c])
+            t = tile([P, N // P, COLS], F32, "raw%d" % (2 + c))
             nc.sync.dma_start(t[:], cap[:, COLS * c : COLS * (c + 1)].rearrange("(n p) m -> p n m", p=P))
             caps.append(t)
         w4_codes = tile([P, HALVES, N], U32, "h1")
         nc.sync.dma_start(w4_codes[:].bitcast(I32), w4_words.rearrange("a p c i -> p a (c i)").bitcast(I32))
 
-        picked_tags = ["big2", "pk0", "pk1", "big3", "wbf0", "wbf2", "wbf1", "big3"]
+        picked_tags = ["wbf1", "u0", "big3", "pk0", "big2", "wbf0", "wbf2", "wbf3"]
         scores = {}
         count = 0
         for b in range(HALVES):
-            planes = tile([P, PACK, M], BF16, "big%d" % b)
+            planes = tile([P, PACK, M], BF16, "raw%d" % b)
             for t in range(PACK):
                 s = PACK * b + t
                 nc.vector.tensor_tensor(pages[s][:].indirect(idx4[:]), h2[s][:], wg2_sb[:, t, :], ALU.mult)
@@ -298,7 +357,7 @@ def tile_list_sawmill_slot_scores_kernel(
                     nc.vector.tensor_copy(
                         picked[:, part], pages[s][:].indirect(idx5[:, part.start // 16 : part.stop // 16])
                     )
-                    act = tile([P, part.stop - part.start], F32, ("r1", "big2")[count % 2])
+                    act = tile([P, part.stop - part.start], F32, ("whole", "wbf1")[count % 2])
                     count = count + 1
                     nc.scalar.activation(act[:], picked[:, part], ACT.Gelu_apprx_tanh)
                     nc.scalar.activation(planes[:, t, part], act[:], ACT.Copy, scale=gain_sb[:, b, t : t + 1])

import math
from contextlib import ExitStack

import concourse.mybir as mybir
from concourse.masks import make_identity

K, T, S, T2, H, M, N = 1024, 2048, 512, 2048, 1024, 1024, 512
FLOPS = 2 * K * H * S * 3 + 2 * H * N * M

F32 = mybir.dt.float32
BF16 = mybir.dt.bfloat16
I32 = mybir.dt.int32
U32 = mybir.dt.uint32
U16 = mybir.dt.uint16
U8 = mybir.dt.uint8
FP8X4 = mybir.dt.float8_e4m3fn_x4
FP4X4 = mybir.dt.float4_e2m1fn_x4
ACT = mybir.ActivationFunctionType
ALU = mybir.AluOpType

P = 128
PACK = 4
PASS = P * PACK
PASSES = K // PASS
HALVES = H // PASS
TILES = H // P
COLS = 512
CHUNKS = M // COLS
ROUNDER = 1.5 * 2.0**23
TWO_PI = 2.0 * math.pi


def tile_list_sawmill_slot_scores_kernel(
    tc, tab_words, tab_scales, tab2_words, tab2_scales, offs, offs2, offs3, offs4, offs5,
    w1_words, w1_scales, b1, w2, w3, wg1, wg2, page0, gain, w4_words, w4_scales, cap, out,
):
    nc = tc.nc
    with ExitStack() as ctx:
        lists = ctx.enter_context(tc.tile_pool(name="lists", bufs=1))
        sb = ctx.enter_context(tc.tile_pool(name="sb", bufs=1))
        ps = ctx.enter_context(tc.psum_pool(name="ps", bufs=1))

        def tile(shape, dtype, tag):
            return sb.tile(shape, dtype, tag=tag, name=tag, align_bytes=64)

        def bank(i):
            return ps.tile([P, COLS], F32, tag="bank%d" % i, name="bank%d" % i)

        def load_list(src, name):
            t = lists.tile(list(src.shape), U16, name=name)
            nc.sync.dma_start(t[:], src)
            return t

        def load_words(words, a, tag):
            t = tile([P, words.shape[2]], I32, tag)
            nc.sync.dma_start(t[:], words[a].rearrange("p c i -> p (c i)").bitcast(I32))
            return t

        def load_planes_side_by_side(queue, planes, scales):
            for q in range(4):
                queue.dma_start(
                    planes[32 * q : 32 * q + 4, :].bitcast(I32).rearrange("r (a c) -> r a c", a=PASSES),
                    scales[:, 4 * q : 4 * q + 4, :].bitcast(I32).rearrange("a r c -> r a c"),
                )

        def load_planes_packed(planes, scales, q):
            nc.sync.dma_start(
                planes[32 * q : 32 * q + 4 * PASSES, :].bitcast(I32),
                scales[:, 4 * q : 4 * q + 4, :].bitcast(I32),
            )

        def load_wg(wg, tag):
            t = tile([P, S], F32, tag)
            nc.sync.dma_start(t[:], wg)
            return t

        def deal_wg(rows, tag, first_bank):
            turned = bank(first_bank)
            for jb in range(PACK):
                nc.tensor.transpose(turned[:, P * jb : P * (jb + 1)], rows[:, P * jb : P * (jb + 1)], ident[:])
            spread = tile([P, PACK, PACK, P], F32, "turns")
            for t in range(PACK):
                nc.scalar.copy(
                    spread[:, t].rearrange("p jb (a q) -> p jb a q", a=4),
                    turned[:].rearrange("p (jb q t) -> p t jb q", jb=PACK, t=PACK)[:, t].unsqueeze(2).to_broadcast([P, PACK, 4, 32]),
                )
            dealt = tile([P, PACK, S], F32, tag)
            for t in range(PACK):
                back = bank((first_bank + 1 + t) % 8)
                for jb in range(PACK):
                    nc.tensor.transpose(back[:, P * jb : P * (jb + 1)], spread[:, t, jb, :], ident[:])
                nc.scalar.copy(dealt[:, t, :], back[:])
            return dealt

        def load_per_row(vec, tag):
            t = tile([P, HALVES, PACK], F32, tag)
            nc.sync.dma_start(t[:], vec.rearrange("(b p t) -> p b t", b=HALVES, t=PACK))
            return t

        def load_page(s, tag):
            b, t = divmod(s, PACK)
            pg = tile([P, T2], F32, tag)
            nc.sync.dma_start(pg[:], page0[PASS * b : PASS * (b + 1), :].rearrange("(p t) c -> p t c", t=PACK)[:, t, :])
            return pg

        ident = tile([P, P], F32, "ident")
        make_identity(nc, ident[:])
        warm = tile([P, 1], F32, "warm")
        nc.scalar.activation(warm[:], ident[:, 0:1], ACT.Sigmoid)
        tab_planes = tile([P, PASSES * T], U8, "x4a")
        nc.vector.memset(tab_planes[:].bitcast(I32), 0)
        w1_planes = tile([P, PASSES * H], U8, "w1s")
        nc.vector.memset(w1_planes[:].bitcast(I32), 0)
        tab2_planes = tile([P, T], U8, "tab2s")
        nc.vector.memset(tab2_planes[:].bitcast(I32), 0)
        w4_planes = tile([P, N], U8, "w4s")
        nc.vector.memset(w4_planes[:].bitcast(I32), 0)

        idx = load_list(offs, "idx")
        wg1_rows = load_wg(wg1, "wg1n")
        tab = [load_words(tab_words, 0, "big0")]
        load_planes_side_by_side(nc.sync, tab_planes, tab_scales)

        def load_w1(b, tag):
            t = tile([P, PASSES * 2 * PASS], U8, tag)
            nc.sync.dma_start(
                t[:].bitcast(I32).rearrange("p (a c) -> p a c", a=PASSES),
                w1_words[:, :, 2 * PASS * b : 2 * PASS * (b + 1)].bitcast(I32).rearrange("a p c -> p a c"),
            )
            return t

        w1_raw = [load_w1(0, "x4b")]
        tab.append(load_words(tab_words, 1, "big1"))
        load_planes_side_by_side(nc.sync, w1_planes, w1_scales)
        b1_sb = load_per_row(b1, "b1")
        idx3 = load_list(offs3, "idx3")
        pages = [load_page(0, "page0")]
        w1_raw.append(load_w1(1, "pk0"))
        wg1_sb = deal_wg(wg1_rows, "wg1", 0)

        def gather_words(windows, offsets, name):
            g = tile([P, PASSES * S], U32, name)
            for a in range(PASSES):
                nc.vector.tensor_copy(g[:, S * a : S * (a + 1)], windows[a][:].bitcast(U32).indirect(offsets[:]))
            return g

        w1_codes = tile([P, HALVES, PASSES, 2 * PASS], U8, "wbf0")
        w1_bytes = tile([P, HALVES, PASSES, PASS], U8, "wbf2")

        def deal_w1(b):
            nc.vector.tensor_copy(
                w1_codes[:, b].bitcast(U16).rearrange("p a (t m) -> p a t m", t=PACK),
                w1_raw[b][:].bitcast(U16).rearrange("p (a m t) -> p a t m", a=PASSES, t=PACK),
            )
            nc.vector.tensor_copy(
                w1_bytes[:, b].rearrange("p a (t m) -> p a t m", t=PACK),
                w1_planes[:].rearrange("p (a b m t) -> p b a t m", a=PASSES, b=HALVES, t=PACK)[:, b],
            )

        deal_w1(0)
        v_words = gather_words(tab, idx, "wbf1")
        v_planes = []
        for a in range(PASSES):
            g = tile([P, S], U8, "vs%d" % a)
            nc.vector.tensor_copy(g[:], tab_planes[:, a * T : (a + 1) * T].indirect(idx[:]))
            v_planes.append(g)
        deal_w1(1)

        h1, f1s = {}, []
        for s in range(TILES):
            b, t = divmod(s, PACK)
            f1 = bank((s + 5) % 8)
            for a in range(PASSES):
                nc.tensor.matmul_mx(
                    f1[:],
                    lhsT=w1_codes[:, b, a, 2 * P * t : 2 * P * (t + 1)].bitcast(FP4X4),
                    lhsT_scale=w1_bytes[:, b, a, P * t : P * (t + 1)],
                    rhs=v_words[:, S * a : S * (a + 1)].bitcast(FP8X4),
                    rhs_scale=v_planes[a][:],
                    start=(a == 0),
                    stop=(a == PASSES - 1),
                )
            f1s.append(f1)

        def profile_features(s, tag):
            b, t = divmod(s, PACK)
            h = tile([P, S], F32, tag)
            nc.scalar.activation(h[:], f1s[s][:], ACT.Sigmoid, bias=b1_sb[:, b, t : t + 1])
            h1[s] = h

        for s in (0, 1, 2, 4, 5, 6, 7):
            profile_features(s, "h%d" % s)

        def put_h1(s):
            nc.vector.tensor_tensor(pages[s][:].indirect(idx3[:]), h1[s][:], wg1_sb[:, s % PACK, :], ALU.mult)

        def load_raw(w, a, b, tag):
            raw = tile([P, PACK, PASS], F32, tag)
            nc.sync.dma_start(
                raw[:], w[PASS * a : PASS * (a + 1), PASS * b : PASS * (b + 1)].rearrange("(p j) c -> p j c", j=PACK)
            )
            return raw

        def quantise_weight(raw, slot, name, dealt):
            rounded = tile([P, PASS * PACK], BF16, "wbf%d" % slot)
            if dealt:
                nc.scalar.copy(
                    rounded[:].rearrange("p (t m j) -> p m t j", t=PACK, j=PACK),
                    raw[:].rearrange("p j (m t) -> p m t j", t=PACK),
                )
            else:
                nc.scalar.copy(
                    rounded[:].rearrange("p (c i j) -> p c j i", i=4, j=PACK),
                    raw[:].rearrange("p j (c i) -> p c j i", i=4),
                )
            codes = tile([P, PASS], U32, name + "c")
            plane = tile([P, PASS], U8, name + "s")
            nc.vector.quantize_mx(codes[:].bitcast(FP8X4), plane[:], rounded[:])
            return codes, plane

        def product(acc, weight, t):
            for a in range(PASSES):
                codes, plane = weight[a]
                nc.tensor.matmul_mx(
                    acc[:],
                    lhsT=codes[:, P * t : P * (t + 1)].bitcast(FP8X4),
                    lhsT_scale=plane[:, P * t : P * (t + 1)],
                    rhs=v2_words[:, S * a : S * (a + 1)].bitcast(FP8X4),
                    rhs_scale=v2_planes[4 * a : P, :],
                    start=(a == 0),
                    stop=(a == PASSES - 1),
                )

        sine_tags = ["h0", "g1", "g2", "h3", "h4", "h5", "h6", "h7"]

        def sines(b, w2q):
            turns = tile([P, PACK, PACK, P], F32, "turns")
            whole = tile([P, PACK, PACK, P], F32, "whole")
            for jb in range(PACK):
                ang = bank(jb)
                for a in range(PASSES):
                    codes, plane = w2q[a]
                    nc.tensor.matmul_mx(
                        ang[:],
                        lhsT=v2_words[:, S * a + P * jb : S * a + P * (jb + 1)].bitcast(FP8X4),
                        lhsT_scale=v2_planes[4 * a : P, P * jb : P * (jb + 1)],
                        rhs=codes[:].bitcast(FP8X4),
                        rhs_scale=plane[:],
                        start=(a == 0),
                        stop=(a == PASSES - 1),
                    )
                nc.scalar.activation(
                    turns[:, jb], ang[:].rearrange("p (m t) -> p t m", t=PACK), ACT.Copy, scale=1.0 / TWO_PI
                )
                shifted = tile([P, PACK, P], U32, "u%d" % (jb % 2))
                nc.scalar.activation(shifted[:], turns[:, jb], ACT.Copy, bias=ROUNDER)
                nc.scalar.activation(whole[:, jb], shifted[:], ACT.Copy, bias=ROUNDER, scale=-1.0)
            got = []
            for t in range(PACK):
                rest = bank(t)
                for jb in range(PACK):
                    for k, term in enumerate((turns, whole)):
                        nc.tensor.matmul(
                            rest[:, P * jb : P * (jb + 1)], lhsT=term[:, jb, t, :], rhs=ident[:],
                            start=(k == 0), stop=(k == 1), is_transpose=True,
                        )
                sine = tile([P, S], F32, sine_tags[PACK * b + t])
                nc.scalar.activation(sine[:], rest[:], ACT.Sin, scale=TWO_PI)
                got.append(sine)
            return got

        h2 = {}

        def extents(w3q, first_bank):
            got = []
            for t in range(PACK):
                ext = bank(first_bank + t)
                product(ext, w3q, t)
                got.append(ext)
            return got

        def knot_features(s, ext, sine, tag=None):
            h2[s] = sine if tag is None else tile([P, S], F32, tag)
            nc.vector.tensor_tensor(h2[s][:], ext[:], sine[:], ALU.mult)

        put_h1(0)
        load_planes_packed(tab2_planes, tab2_scales, 0)
        pages.append(load_page(1, "page1"))
        put_h1(1)
        wg2_rows = load_wg(wg2, "wg2n")
        wg2_sb = deal_wg(wg2_rows, "wg2", 4)
        load_planes_packed(tab2_planes, tab2_scales, 1)
        pages.append(load_page(2, "page2"))
        put_h1(2)
        idx2 = load_list(offs2, "idx2")
        load_planes_packed(tab2_planes, tab2_scales, 2)
        tab2 = [load_words(tab2_words, 0, "big2")]
        load_planes_packed(tab2_planes, tab2_scales, 3)
        tab2.append(load_words(tab2_words, 1, "big3"))
        v2_words = gather_words(tab2, idx2, "h1")
        v2_planes = tile([P, S], U8, "h2")
        nc.vector.tensor_copy(v2_planes[:], tab2_planes[:].indirect(idx2[:]))

        raw2 = [load_raw(w2, a, 0, "raw%d" % a) for a in range(PASSES)]
        pages.append(load_page(3, "page3"))
        pages.append(load_page(4, "page4"))
        raw3 = [load_raw(w3, 0, 0, "raw2")]
        pages.append(load_page(5, "page5"))
        raw3.append(load_raw(w3, 1, 0, "raw3"))
        pages.append(load_page(6, "big0"))
        idx4 = load_list(offs4, "idx4")
        pages.append(load_page(7, "big1"))
        idx5 = load_list(offs5, "idx5")
        w2q = [quantise_weight(raw2[a], a, "w2q0%d" % a, False) for a in range(PASSES)]
        profile_features(3, "wbf0")
        sine = sines(0, w2q)
        put_h1(3)
        put_h1(4)
        w3q = [quantise_weight(raw3[a], (2, 1)[a], "w3q0%d" % a, True) for a in range(PASSES)]
        for s in range(5, TILES):
            put_h1(s)
        ext = extents(w3q, PACK)
        knot_features(0, ext[0], sine[0])
        knot_features(1, ext[1], sine[1])
        raw2 = [load_raw(w2, a, 1, "raw%d" % a) for a in range(PASSES)]
        gain_sb = load_per_row(gain, "gain")
        raw3 = [load_raw(w3, a, 1, "raw%d" % (2 + a)) for a in range(PASSES)]
        w2q = [quantise_weight(raw2[a], (0, 2)[a], "w2q1%d" % a, False) for a in range(PASSES)]
        knot_features(2, ext[2], sine[2], "wbf2")
        w3q = [quantise_weight(raw3[a], (1, 3)[a], "w3q1%d" % a, True) for a in range(PASSES)]
        knot_features(3, ext[3], sine[3], "wbf3")
        sine = sines(1, w2q)
        ext = extents(w3q, 0)
        for t in range(PACK):
            knot_features(PACK + t, ext[t], sine[t])
        for q in range(4):
            load_planes_packed(w4_planes, w4_scales, q)
        caps = []
        for c in range(CHUNKS):
            t = tile([P, N // P, COLS], F32, "raw%d" % (2 + c))
            nc.sync.dma_start(t[:], cap[:, COLS * c : COLS * (c + 1)].rearrange("(n p) m -> p n m", p=P))
            caps.append(t)
        w4_codes = tile([P, HALVES, N], U32, "h1")
        nc.sync.dma_start(w4_codes[:].bitcast(I32), w4_words.rearrange("a p c i -> p a (c i)").bitcast(I32))

        picked_tags = ["wbf1", "u0", "big3", "pk0", "big2", "wbf0", "wbf2", "wbf3"]
        scores = {}
        count = 0
        for b in range(HALVES):
            planes = tile([P, PACK, M], BF16, "raw%d" % b)
            for t in range(PACK):
                s = PACK * b + t
                nc.vector.tensor_tensor(pages[s][:].indirect(idx4[:]), h2[s][:], wg2_sb[:, t, :], ALU.mult)
                picked = tile([P, M], F32, picked_tags[s])
                parts = [slice(0, M)] if s < TILES - 1 else [slice(COLS * c, COLS * (c + 1)) for c in range(CHUNKS)]
                for part in parts:
                    nc.vector.tensor_copy(
                        picked[:, part], pages[s][:].indirect(idx5[:, part.start // 16 : part.stop // 16])
                    )
                    act = tile([P, part.stop - part.start], F32, ("whole", "wbf1")[count % 2])
                    count = count + 1
                    nc.scalar.activation(act[:], picked[:, part], ACT.Gelu_apprx_tanh)
                    nc.scalar.activation(planes[:, t, part], act[:], ACT.Copy, scale=gain_sb[:, b, t : t + 1])
            for c in range(CHUNKS):
                woven = tile([P, COLS * PACK], BF16, ("x4a", "x4b")[c])
                dst = woven[:].rearrange("p (c i t) -> p c t i", i=4, t=PACK)
                src = planes[:, :, COLS * c : COLS * (c + 1)].rearrange("p t (c i) -> p c t i", i=4)
                if b == HALVES - 1 and c == 0:
                    nc.vector.tensor_copy(dst, src)
                else:
                    nc.scalar.copy(dst, src)
                name = "w%dq0%d" % (2 + b, c)
                codes = tile([P, COLS], U32, name + "c")
                plane = tile([P, COLS], U8, name + "s")
                nc.vector.quantize_mx(codes[:].bitcast(FP8X4), plane[:], woven[:])
                for n in range(N // P):
                    if b == 0:
                        scores[c, n] = bank(PACK * c + n)
                    nc.tensor.matmul_mx(
                        scores[c, n][:],
                        lhsT=w4_codes[:, b, P * n : P * (n + 1)].bitcast(FP8X4),
                        lhsT_scale=w4_planes[4 * b : P, P * n : P * (n + 1)],
                        rhs=codes[:].bitcast(FP8X4),
                        rhs_scale=plane[:],
                        start=(b == 0),
                        stop=(b == HALVES - 1),
                    )
                    if b == HALVES - 1:
                        nc.vector.tensor_tensor(caps[c][:, n, :], scores[c, n][:], caps[c][:, n, :], ALU.min)
                        nc.sync.dma_start(out[P * n : P * (n + 1), COLS * c : COLS * (c + 1)], caps[c][:, n, :])
